import numpy as np
import ml_dtypes


def mxq(x, axis, fmt="e4m3"):
    dtype, down = {"e4m3": (ml_dtypes.float8_e4m3fn, 7), "e5m2": (ml_dtypes.float8_e5m2, 14)}[fmt]
    v = np.moveaxis(np.asarray(x, np.float32).astype(ml_dtypes.bfloat16).astype(np.float64), axis, -1)
    blocks = v.reshape(v.shape[:-1] + (-1, 32))
    amax = np.abs(blocks).max(-1, keepdims=True)
    byte = np.maximum(np.where(amax > 0, np.frexp(amax)[1] - 1 + 127, 0) - down, 1)
    scale = np.exp2(byte - 127.0)
    codes = (blocks / scale).astype(np.float32).astype(dtype).astype(np.float64)
    return np.moveaxis((codes * scale).reshape(v.shape), -1, axis)


WIDE = False


def mx_kscale(k, group=512):
    if not WIDE:
        return np.ones(k)
    levels = np.array([10, -10, 5, -5, 0])
    if group != 512:
        return np.exp2(np.random.permutation(np.resize(levels, k // group))).repeat(group)
    if k % 512:
        return np.exp2(np.random.permutation(np.resize(levels, k // 32))).repeat(32)
    a = np.empty((k // 512, 16))
    for p in range(k // 512):
        a[p, :8] = np.random.permutation(np.resize(levels, 8))
        for g in range(8):
            far = levels[np.abs(levels - a[p, g]) >= 10]
            a[p, g + 8] = far[np.random.randint(len(far))]
    return np.exp2(a.ravel()).repeat(32)


def f64(x):
    return np.asarray(x).astype(np.float64)


G, D, M, N = 4, 256, 256, 512


def setup_inputs():
    n = np.random.standard_normal
    s = mx_kscale(D, 0)[:, None]
    return {
        "x": (n((G, D, N)) * s).astype(np.float32),
        "w": (n((G, D, M)) / np.sqrt(D) / s).astype(np.float32),
        "b": (0.5 * n((G, M, 1))).astype(np.float32),
    }


def reference(x, w, b):
    xq = mxq(f64(x), 1, "e4m3")
    y = mxq(f64(w), 1, "e4m3").transpose(0, 2, 1) @ xq
    y = y + f64(b)
    y = np.tanh(y)
    return y

@@ -1,0 +1,146 @@
+from contextlib import ExitStack
+
+import concourse.mybir as mybir
+
+G, D, M, N = 4, 256, 256, 512
+FLOPS = 2 * G * D * M * N
+
+F32 = mybir.dt.float32
+BF16 = mybir.dt.bfloat16
+U32 = mybir.dt.uint32
+U8 = mybir.dt.uint8
+FP8X4 = mybir.dt.float8_e4m3fn_x4
+TANH = mybir.ActivationFunctionType.Tanh
+
+P = 128
+PACK = 4
+ROWS = D // PACK
+SIDE = P // ROWS
+PAIRS = G // SIDE
+M_TILE = 128
+M_TILES = M // M_TILE
+HALF = N // 2
+QUAD = 32
+LINE = 4
+
+
+def tile_rows_glin_tanh_bias_kernel(tc, x, w, b, out):
+    nc = tc.nc
+    x_rows = x.rearrange("g (p j) n -> (g p) j n", j=PACK)
+    w_rows = w.rearrange("g (p j) m -> (g p) j m", j=PACK)
+
+    with ExitStack() as ctx:
+        sb = ctx.enter_context(tc.tile_pool(name="sb", bufs=1))
+        psum = ctx.enter_context(tc.psum_pool(name="psum", bufs=1))
+        ctx.enter_context(tc.manual_schedule())
+
+        def tiles(name, count, shape, dtype):
+            return [sb.tile(shape, dtype, name="%s%d" % (name, i), align_bytes=64) for i in range(count)]
+
+        x_raw = tiles("x_raw", PAIRS, [P, PACK, N], F32)
+        w_raw = tiles("w_raw", PAIRS, [P, PACK, M], F32)
+        x_bf = tiles("x_bf", PAIRS * 2, [P, HALF, PACK], BF16)
+        w_bf = tiles("w_bf", PAIRS * M_TILES, [P, M_TILE, PACK], BF16)
+        x_codes = tiles("x_codes", PAIRS, [P, N], U32)
+        x_scales = tiles("x_scales", PAIRS, [P, N], U8)
+        w_codes = tiles("w_codes", PAIRS * M_TILES, [P, M_TILE], U32)
+        w_scales = tiles("w_scales", PAIRS * M_TILES, [P, M_TILE], U8)
+        result = tiles("result", G * M_TILES, [P, N], F32)
+        bias_rows = sb.tile([P, G * M_TILES * QUAD], F32, align_bytes=64)
+        bias_cols = sb.tile([P, G * M_TILES * QUAD], F32, align_bytes=64)
+        acc = [psum.tile([M_TILE, N], F32, name="acc%d" % i) for i in range(G * M_TILES)]
+
+        nc.vector.memset(bias_rows[:], 0.0)
+        nc.sync.dma_start(out=x_raw[0][:], in_=x_rows[0:P])
+        nc.sync.dma_start(
+            out=bias_rows[0:P:QUAD, :].rearrange("a (c i) -> a c i", i=QUAD),
+            in_=b.rearrange("g (h a i) o -> a (g h) (i o)", h=M_TILES, i=QUAD),
+        )
+        nc.sync.dma_start(out=w_raw[0][:], in_=w_rows[0:P])
+        nc.sync.dma_start(out=x_raw[1][:], in_=x_rows[P : 2 * P])
+        nc.sync.dma_start(out=w_raw[1][:], in_=w_rows[P : 2 * P])
+
+        def interleave(copy, dst, src):
+            copy(
+                out=dst.rearrange("p (c i) t -> p c t i", i=LINE),
+                in_=src.rearrange("p t (c i) -> p c t i", i=LINE),
+            )
+
+        def round_x(copy, s, lo, hi):
+            half = lo // HALF
+            interleave(copy, x_bf[2 * s + half][:, lo - half * HALF : hi - half * HALF, :], x_raw[s][:, :, lo:hi])
+
+        def round_w(copy, s, h):
+            interleave(copy, w_bf[s * M_TILES + h][:], w_raw[s][:, :, h * M_TILE : (h + 1) * M_TILE])
+
+        def quantize_x(s, half):
+            cols = slice(half * HALF, (half + 1) * HALF)
+            nc.vector.quantize_mx(
+                out=x_codes[s][:, cols].bitcast(FP8X4),
+                scales=x_scales[s][:, cols],
+                in_=x_bf[2 * s + half][:].rearrange("p n t -> p (n t)"),
+            )
+
+        def quantize_w(s, h):
+            i = s * M_TILES + h
+            nc.vector.quantize_mx(
+                out=w_codes[i][:].bitcast(FP8X4),
+                scales=w_scales[i][:],
+                in_=w_bf[i][:].rearrange("p m t -> p (m t)"),
+            )
+
+        def multiply(s, h):
+            i = s * M_TILES + h
+            for c in range(SIDE):
+                rows = slice(c * ROWS, (c + 1) * ROWS)
+                nc.tensor.matmul_mx(
+                    out=acc[(s * SIDE + c) * M_TILES + h][:],
+                    lhsT=w_codes[i][rows, :].bitcast(FP8X4),
+                    lhsT_scale=w_scales[i][rows, :],
+                    rhs=x_codes[s][rows, :].bitcast(FP8X4),
+                    rhs_scale=x_scales[s][rows, :],
+                    start=True,
+                    stop=True,
+                )
+
+        def finish(g, h):
+            i = g * M_TILES + h
+            nc.scalar.activation(
+                out=result[i][:], in_=acc[i][:], func=TANH, bias=bias_cols[:, i * QUAD : i * QUAD + 1]
+            )
+            nc.sync.dma_start(out=out[g, h * M_TILE : (h + 1) * M_TILE, :], in_=result[i][:])
+
+        on_vector = nc.vector.tensor_copy
+        on_scalar = nc.scalar.copy
+
+        round_x(on_vector, 0, 0, 256)
+        round_x(on_scalar, 0, 352, 512)
+        round_x(on_vector, 0, 256, 352)
+        quantize_x(0, 0)
+        nc.vector.transpose(bias_cols[:], bias_rows[:])
+        quantize_x(0, 1)
+        round_w(on_scalar, 0, 0)
+        round_w(on_vector, 0, 1)
+        quantize_w(0, 0)
+        quantize_w(0, 1)
+        multiply(0, 0)
+        multiply(0, 1)
+        finish(0, 0)
+        round_x(on_vector, 1, 0, 256)
+        round_x(on_scalar, 1, 384, 512)
+        round_x(on_vector, 1, 256, 384)
+        finish(1, 0)
+        finish(0, 1)
+        finish(1, 1)
+        quantize_x(1, 0)
+        round_w(on_vector, 1, 0)
+        quantize_x(1, 1)
+        quantize_w(1, 0)
+        multiply(1, 0)
+        round_w(on_vector, 1, 1)
+        quantize_w(1, 1)
+        multiply(1, 1)
+        finish(2, 0)
+        finish(3, 0)
+        finish(2, 1)
+        finish(3, 1)

@@ -20,6 +20,8 @@ PAIRS = G // SIDE
 M_TILE = 128
 M_TILES = M // M_TILE
 HALF = N // 2
+N_TILE = 128
+N_TILES = N // N_TILE
 QUAD = 32
 LINE = 4
 
@@ -89,26 +91,30 @@ def tile_rows_glin_tanh_bias_kernel(tc, x, w, b, out):
                 in_=w_bf[i][:].rearrange("p m t -> p (m t)"),
             )
 
-        def multiply(s, h):
+        def multiply(bank, g, h, q):
+            s, c = divmod(g, SIDE)
             i = s * M_TILES + h
-            for c in range(SIDE):
-                rows = slice(c * ROWS, (c + 1) * ROWS)
-                nc.tensor.matmul_mx(
-                    out=acc[(s * SIDE + c) * M_TILES + h][:],
-                    lhsT=w_codes[i][rows, :].bitcast(FP8X4),
-                    lhsT_scale=w_scales[i][rows, :],
-                    rhs=x_codes[s][rows, :].bitcast(FP8X4),
-                    rhs_scale=x_scales[s][rows, :],
-                    start=True,
-                    stop=True,
-                )
+            rows = slice(c * ROWS, (c + 1) * ROWS)
+            cols = slice(q * N_TILE, (q + 1) * N_TILE)
+            nc.tensor.matmul_mx(
+                out=bank[:, cols],
+                lhsT=w_codes[i][rows, :].bitcast(FP8X4),
+                lhsT_scale=w_scales[i][rows, :],
+                rhs=x_codes[s][rows, cols].bitcast(FP8X4),
+                rhs_scale=x_scales[s][rows, cols],
+                start=True,
+                stop=True,
+            )
 
-        def finish(g, h):
+        def finish(bank, g, h, lo, hi):
             i = g * M_TILES + h
             nc.scalar.activation(
-                out=result[i][:], in_=acc[i][:], func=TANH, bias=bias_cols[:, i * QUAD : i * QUAD + 1]
+                out=result[i][:, lo:hi], in_=bank[:, lo:hi], func=TANH, bias=bias_cols[:, i * QUAD : i * QUAD + 1]
             )
-            nc.sync.dma_start(out=out[g, h * M_TILE : (h + 1) * M_TILE, :], in_=result[i][:])
+            nc.sync.dma_start(out=out[g, h * M_TILE : (h + 1) * M_TILE, lo:hi], in_=result[i][:, lo:hi])
+
+        def own(g, h):
+            return acc[g * M_TILES + h]
 
         on_vector = nc.vector.tensor_copy
         on_scalar = nc.scalar.copy
@@ -117,30 +123,39 @@ def tile_rows_glin_tanh_bias_kernel(tc, x, w, b, out):
         round_x(on_scalar, 0, 352, 512)
         round_x(on_vector, 0, 256, 352)
         quantize_x(0, 0)
-        nc.vector.transpose(bias_cols[:], bias_rows[:])
+        round_w(on_vector, 0, 0)
         quantize_x(0, 1)
-        round_w(on_scalar, 0, 0)
-        round_w(on_vector, 0, 1)
+        round_w(on_scalar, 0, 1)
         quantize_w(0, 0)
+        nc.vector.transpose(bias_cols[:], bias_rows[:])
         quantize_w(0, 1)
-        multiply(0, 0)
-        multiply(0, 1)
-        finish(0, 0)
+        for h in range(M_TILES):
+            for g in (0, 1):
+                for q in range(N_TILES):
+                    multiply(own(g, h), g, h, q)
+        finish(own(0, 0), 0, 0, 0, N)
         round_x(on_vector, 1, 0, 256)
         round_x(on_scalar, 1, 384, 512)
         round_x(on_vector, 1, 256, 384)
-        finish(1, 0)
-        finish(0, 1)
-        finish(1, 1)
+        finish(own(1, 0), 1, 0, 0, N)
+        finish(own(0, 1), 0, 1, 0, N)
+        finish(own(1, 1), 1, 1, 0, N)
         quantize_x(1, 0)
         round_w(on_vector, 1, 0)
         quantize_x(1, 1)
         quantize_w(1, 0)
-        multiply(1, 0)
+        for q in range(N_TILES):
+            multiply(own(2, 0) if q < 2 else own(0, 0), 2, 0, q)
+        for q in range(N_TILES):
+            multiply(own(3, 0), 3, 0, q)
         round_w(on_vector, 1, 1)
         quantize_w(1, 1)
-        multiply(1, 1)
-        finish(2, 0)
-        finish(3, 0)
-        finish(2, 1)
-        finish(3, 1)
+        for g in (2, 3):
+            for q in range(N_TILES):
+                multiply(own(g, 1), g, 1, q)
+        finish(own(2, 0), 2, 0, 0, HALF)
+        finish(own(0, 0), 2, 0, HALF, N)
+        finish(own(3, 0), 3, 0, 0, N)
+        finish(own(2, 1), 2, 1, 0, N)
+        finish(own(3, 1), 3, 1, 0, HALF)
+        finish(own(3, 1), 3, 1, HALF, N)

@@ -39,9 +39,11 @@ def tile_rows_glin_tanh_bias_kernel(tc, x, w, b, out):
         def tiles(name, count, shape, dtype):
             return [sb.tile(shape, dtype, name="%s%d" % (name, i), align_bytes=64) for i in range(count)]
 
-        x_raw = tiles("x_raw", PAIRS, [P, PACK, N], F32)
+        x_first = sb.tile([P, PACK, N], F32)
+        x_last = tiles("x_last", 2, [P, PACK, HALF], F32)
+        x_last_bf = tiles("x_last_bf", N_TILES, [P, N_TILE, PACK], BF16)
         w_raw = tiles("w_raw", PAIRS, [P, PACK, M], F32)
-        x_bf = tiles("x_bf", PAIRS * 2, [P, HALF, PACK], BF16)
+        x_bf = tiles("x_bf", 2, [P, HALF, PACK], BF16)
         w_bf = tiles("w_bf", PAIRS * M_TILES, [P, M_TILE, PACK], BF16)
         x_codes = tiles("x_codes", PAIRS, [P, N], U32)
         x_scales = tiles("x_scales", PAIRS, [P, N], U8)
@@ -53,14 +55,15 @@ def tile_rows_glin_tanh_bias_kernel(tc, x, w, b, out):
         acc = [psum.tile([M_TILE, N], F32, name="acc%d" % i) for i in range(G * M_TILES)]
 
         nc.vector.memset(bias_rows[:], 0.0)
-        nc.sync.dma_start(out=x_raw[0][:], in_=x_rows[0:P])
+        nc.sync.dma_start(out=x_first[:], in_=x_rows[0:P])
         nc.sync.dma_start(
             out=bias_rows[0:P:QUAD, :].rearrange("a (c i) -> a c i", i=QUAD),
             in_=b.rearrange("g (h a i) o -> a (g h) (i o)", h=M_TILES, i=QUAD),
         )
         nc.sync.dma_start(out=w_raw[0][:], in_=w_rows[0:P])
-        nc.sync.dma_start(out=x_raw[1][:], in_=x_rows[P : 2 * P])
         nc.sync.dma_start(out=w_raw[1][:], in_=w_rows[P : 2 * P])
+        for half in range(2):
+            nc.sync.dma_start(out=x_last[half][:], in_=x_rows[P : 2 * P, :, half * HALF : (half + 1) * HALF])
 
         def interleave(copy, dst, src):
             copy(
@@ -70,7 +73,7 @@ def tile_rows_glin_tanh_bias_kernel(tc, x, w, b, out):
 
         def round_x(copy, s, lo, hi):
             half = lo // HALF
-            interleave(copy, x_bf[2 * s + half][:, lo - half * HALF : hi - half * HALF, :], x_raw[s][:, :, lo:hi])
+            interleave(copy, x_bf[2 * s + half][:, lo - half * HALF : hi - half * HALF, :], x_first[:, :, lo:hi])
 
         def round_w(copy, s, h):
             interleave(copy, w_bf[s * M_TILES + h][:], w_raw[s][:, :, h * M_TILE : (h + 1) * M_TILE])
@@ -82,6 +85,21 @@ def tile_rows_glin_tanh_bias_kernel(tc, x, w, b, out):
                 scales=x_scales[s][:, cols],
                 in_=x_bf[2 * s + half][:].rearrange("p n t -> p (n t)"),
             )
+
+        def last_half(half):
+            for k in range(2):
+                interleave(
+                    nc.vector.tensor_copy,
+                    x_last_bf[2 * half + k][:],
+                    x_last[half][:, :, k * N_TILE : (k + 1) * N_TILE],
+                )
+            for q in (2 * half, 2 * half + 1):
+                cols = slice(q * N_TILE, (q + 1) * N_TILE)
+                nc.vector.quantize_mx(
+                    out=x_codes[1][:, cols].bitcast(FP8X4),
+                    scales=x_scales[1][:, cols],
+                    in_=x_last_bf[q][:].rearrange("p n t -> p (n t)"),
+                )
 
         def quantize_w(s, h):
             i = s * M_TILES + h
@@ -111,6 +129,9 @@ def tile_rows_glin_tanh_bias_kernel(tc, x, w, b, out):
             nc.scalar.activation(
                 out=result[i][:, lo:hi], in_=bank[:, lo:hi], func=TANH, bias=bias_cols[:, i * QUAD : i * QUAD + 1]
             )
+
+        def store(g, h, lo, hi):
+            i = g * M_TILES + h
             nc.sync.dma_start(out=out[g, h * M_TILE : (h + 1) * M_TILE, lo:hi], in_=result[i][:, lo:hi])
 
         def own(g, h):
@@ -132,30 +153,30 @@ def tile_rows_glin_tanh_bias_kernel(tc, x, w, b, out):
         for h in range(M_TILES):
             for g in (0, 1):
                 for q in range(N_TILES):
-                    multiply(own(g, h), g, h, q)
-        finish(own(0, 0), 0, 0, 0, N)
-        round_x(on_vector, 1, 0, 256)
-        round_x(on_scalar, 1, 384, 512)
-        round_x(on_vector, 1, 256, 384)
-        finish(own(1, 0), 1, 0, 0, N)
-        finish(own(0, 1), 0, 1, 0, N)
-        finish(own(1, 1), 1, 1, 0, N)
-        quantize_x(1, 0)
-        round_w(on_vector, 1, 0)
-        quantize_x(1, 1)
-        quantize_w(1, 0)
-        for q in range(N_TILES):
-            multiply(own(2, 0) if q < 2 else own(0, 0), 2, 0, q)
-        for q in range(N_TILES):
-            multiply(own(3, 0), 3, 0, q)
-        round_w(on_vector, 1, 1)
-        quantize_w(1, 1)
+                    multiply(own(2, 0) if (g, h) == (0, 0) and q < 2 else own(g, h), g, h, q)
+        finish(own(2, 0), 0, 0, 0, HALF)
+        store(0, 0, 0, HALF)
+        for h in range(M_TILES):
+            for g in (0, 1):
+                lo = HALF if (g, h) == (0, 0) else 0
+                finish(own(g, h), g, h, lo, N)
+                store(g, h, lo, N)
+        for h in range(M_TILES):
+            round_w(on_vector, 1, h)
+        for h in range(M_TILES):
+            quantize_w(1, h)
+        last_half(0)
         for g in (2, 3):
-            for q in range(N_TILES):
-                multiply(own(g, 1), g, 1, q)
-        finish(own(2, 0), 2, 0, 0, HALF)
-        finish(own(0, 0), 2, 0, HALF, N)
-        finish(own(3, 0), 3, 0, 0, N)
-        finish(own(2, 1), 2, 1, 0, N)
-        finish(own(3, 1), 3, 1, 0, HALF)
-        finish(own(3, 1), 3, 1, HALF, N)
+            for h in range(M_TILES):
+                for q in (0, 1):
+                    multiply(own(g, h), g, h, q)
+                finish(own(g, h), g, h, 0, HALF)
+                if g == 2:
+                    store(g, h, 0, HALF)
+        last_half(1)
+        for g in (3, 2):
+            for h in range(M_TILES):
+                for q in (2, 3):
+                    multiply(own(g - SIDE, h), g, h, q)
+                finish(own(g - SIDE, h), g, h, HALF, N)
+                store(g, h, HALF if g == 2 else 0, N)

@@ -171,12 +171,11 @@ def tile_rows_glin_tanh_bias_kernel(tc, x, w, b, out):
                 for q in (0, 1):
                     multiply(own(g, h), g, h, q)
                 finish(own(g, h), g, h, 0, HALF)
-                if g == 2:
-                    store(g, h, 0, HALF)
+                store(g, h, 0, HALF)
         last_half(1)
-        for g in (3, 2):
+        for g in (2, 3):
             for h in range(M_TILES):
                 for q in (2, 3):
                     multiply(own(g - SIDE, h), g, h, q)
                 finish(own(g - SIDE, h), g, h, HALF, N)
-                store(g, h, HALF if g == 2 else 0, N)
+                store(g, h, HALF, N)

from contextlib import ExitStack

import concourse.mybir as mybir

G, D, M, N = 4, 256, 256, 512
FLOPS = 2 * G * D * M * N

F32 = mybir.dt.float32
BF16 = mybir.dt.bfloat16
U32 = mybir.dt.uint32
U8 = mybir.dt.uint8
FP8X4 = mybir.dt.float8_e4m3fn_x4
TANH = mybir.ActivationFunctionType.Tanh

P = 128
PACK = 4
ROWS = D // PACK
SIDE = P // ROWS
PAIRS = G // SIDE
M_TILE = 128
M_TILES = M // M_TILE
HALF = N // 2
N_TILE = 128
N_TILES = N // N_TILE
QUAD = 32
LINE = 4


def tile_rows_glin_tanh_bias_kernel(tc, x, w, b, out):
    nc = tc.nc
    x_rows = x.rearrange("g (p j) n -> (g p) j n", j=PACK)
    w_rows = w.rearrange("g (p j) m -> (g p) j m", j=PACK)

    with ExitStack() as ctx:
        sb = ctx.enter_context(tc.tile_pool(name="sb", bufs=1))
        psum = ctx.enter_context(tc.psum_pool(name="psum", bufs=1))
        ctx.enter_context(tc.manual_schedule())

        def tiles(name, count, shape, dtype):
            return [sb.tile(shape, dtype, name="%s%d" % (name, i), align_bytes=64) for i in range(count)]

        x_first = sb.tile([P, PACK, N], F32)
        x_last = tiles("x_last", 2, [P, PACK, HALF], F32)
        x_last_bf = tiles("x_last_bf", N_TILES, [P, N_TILE, PACK], BF16)
        w_raw = tiles("w_raw", PAIRS, [P, PACK, M], F32)
        x_bf = tiles("x_bf", 2, [P, HALF, PACK], BF16)
        w_bf = tiles("w_bf", PAIRS * M_TILES, [P, M_TILE, PACK], BF16)
        x_codes = tiles("x_codes", PAIRS, [P, N], U32)
        x_scales = tiles("x_scales", PAIRS, [P, N], U8)
        w_codes = tiles("w_codes", PAIRS * M_TILES, [P, M_TILE], U32)
        w_scales = tiles("w_scales", PAIRS * M_TILES, [P, M_TILE], U8)
        result = tiles("result", G * M_TILES, [P, N], F32)
        bias_rows = sb.tile([P, G * M_TILES * QUAD], F32, align_bytes=64)
        bias_cols = sb.tile([P, G * M_TILES * QUAD], F32, align_bytes=64)
        acc = [psum.tile([M_TILE, N], F32, name="acc%d" % i) for i in range(G * M_TILES)]

        nc.vector.memset(bias_rows[:], 0.0)
        nc.sync.dma_start(out=x_first[:], in_=x_rows[0:P])
        nc.sync.dma_start(
            out=bias_rows[0:P:QUAD, :].rearrange("a (c i) -> a c i", i=QUAD),
            in_=b.rearrange("g (h a i) o -> a (g h) (i o)", h=M_TILES, i=QUAD),
        )
        nc.sync.dma_start(out=w_raw[0][:], in_=w_rows[0:P])
        nc.sync.dma_start(out=w_raw[1][:], in_=w_rows[P : 2 * P])
        for half in range(2):
            nc.sync.dma_start(out=x_last[half][:], in_=x_rows[P : 2 * P, :, half * HALF : (half + 1) * HALF])

        def interleave(copy, dst, src):
            copy(
                out=dst.rearrange("p (c i) t -> p c t i", i=LINE),
                in_=src.rearrange("p t (c i) -> p c t i", i=LINE),
            )

        def round_x(copy, s, lo, hi):
            half = lo // HALF
            interleave(copy, x_bf[2 * s + half][:, lo - half * HALF : hi - half * HALF, :], x_first[:, :, lo:hi])

        def round_w(copy, s, h):
            interleave(copy, w_bf[s * M_TILES + h][:], w_raw[s][:, :, h * M_TILE : (h + 1) * M_TILE])

        def quantize_x(s, half):
            cols = slice(half * HALF, (half + 1) * HALF)
            nc.vector.quantize_mx(
                out=x_codes[s][:, cols].bitcast(FP8X4),
                scales=x_scales[s][:, cols],
                in_=x_bf[2 * s + half][:].rearrange("p n t -> p (n t)"),
            )

        def last_half(half):
            for k in range(2):
                interleave(
                    nc.vector.tensor_copy,
                    x_last_bf[2 * half + k][:],
                    x_last[half][:, :, k * N_TILE : (k + 1) * N_TILE],
                )
            for q in (2 * half, 2 * half + 1):
                cols = slice(q * N_TILE, (q + 1) * N_TILE)
                nc.vector.quantize_mx(
                    out=x_codes[1][:, cols].bitcast(FP8X4),
                    scales=x_scales[1][:, cols],
                    in_=x_last_bf[q][:].rearrange("p n t -> p (n t)"),
                )

        def quantize_w(s, h):
            i = s * M_TILES + h
            nc.vector.quantize_mx(
                out=w_codes[i][:].bitcast(FP8X4),
                scales=w_scales[i][:],
                in_=w_bf[i][:].rearrange("p m t -> p (m t)"),
            )

        def multiply(bank, g, h, q):
            s, c = divmod(g, SIDE)
            i = s * M_TILES + h
            rows = slice(c * ROWS, (c + 1) * ROWS)
            cols = slice(q * N_TILE, (q + 1) * N_TILE)
            nc.tensor.matmul_mx(
                out=bank[:, cols],
                lhsT=w_codes[i][rows, :].bitcast(FP8X4),
                lhsT_scale=w_scales[i][rows, :],
                rhs=x_codes[s][rows, cols].bitcast(FP8X4),
                rhs_scale=x_scales[s][rows, cols],
                start=True,
                stop=True,
            )

        def finish(bank, g, h, lo, hi):
            i = g * M_TILES + h
            nc.scalar.activation(
                out=result[i][:, lo:hi], in_=bank[:, lo:hi], func=TANH, bias=bias_cols[:, i * QUAD : i * QUAD + 1]
            )

        def store(g, h, lo, hi):
            i = g * M_TILES + h
            nc.sync.dma_start(out=out[g, h * M_TILE : (h + 1) * M_TILE, lo:hi], in_=result[i][:, lo:hi])

        def own(g, h):
            return acc[g * M_TILES + h]

        on_vector = nc.vector.tensor_copy
        on_scalar = nc.scalar.copy

        round_x(on_vector, 0, 0, 256)
        round_x(on_scalar, 0, 352, 512)
        round_x(on_vector, 0, 256, 352)
        quantize_x(0, 0)
        round_w(on_vector, 0, 0)
        quantize_x(0, 1)
        round_w(on_scalar, 0, 1)
        quantize_w(0, 0)
        nc.vector.transpose(bias_cols[:], bias_rows[:])
        quantize_w(0, 1)
        for h in range(M_TILES):
            for g in (0, 1):
                for q in range(N_TILES):
                    multiply(own(2, 0) if (g, h) == (0, 0) and q < 2 else own(g, h), g, h, q)
        finish(own(2, 0), 0, 0, 0, HALF)
        store(0, 0, 0, HALF)
        for h in range(M_TILES):
            for g in (0, 1):
                lo = HALF if (g, h) == (0, 0) else 0
                finish(own(g, h), g, h, lo, N)
                store(g, h, lo, N)
        for h in range(M_TILES):
            round_w(on_vector, 1, h)
        for h in range(M_TILES):
            quantize_w(1, h)
        last_half(0)
        for g in (2, 3):
            for h in range(M_TILES):
                for q in (0, 1):
                    multiply(own(g, h), g, h, q)
                finish(own(g, h), g, h, 0, HALF)
                store(g, h, 0, HALF)
        last_half(1)
        for g in (2, 3):
            for h in range(M_TILES):
                for q in (2, 3):
                    multiply(own(g - SIDE, h), g, h, q)
                finish(own(g - SIDE, h), g, h, HALF, N)
                store(g, h, HALF, N)
